import numpy as np, ml_dtypes
CORES = [45,53,77,117,47,55,79,119]
N = 8
NH, QP = 8, 128
def setup_inputs(rng):
    return {"q": rng.standard_normal((N, 128, NH * QP), dtype=np.float32).astype(ml_dtypes.bfloat16), "k": rng.standard_normal((N, 128, NH * 128), dtype=np.float32).astype(ml_dtypes.bfloat16), "v": rng.standard_normal((N, 128, NH * 128), dtype=np.float32).astype(ml_dtypes.bfloat16)}
def setup_inputs_big(rng):
    d = setup_inputs(rng)
    for k in ("q", "k", "v"): d[k] = (d[k].astype(np.float32) * 1024.0).astype(d[k].dtype)
    return d
def setup_inputs_small(rng):
    d = setup_inputs(rng)
    for k in ("q", "k", "v"): d[k] = (d[k].astype(np.float32) * (1 / 1024.0)).astype(d[k].dtype)
    return d
def setup_inputs_apart(rng):
    d = setup_inputs(rng)
    f = (10.0 ** rng.permutation(np.linspace(-1.5, 1.5, N))).astype(np.float32).reshape(N, 1, 1)
    for k in ("q", "k", "v"): d[k] = (d[k].astype(np.float32) * f).astype(d[k].dtype)
    return d
def reference(q, k, v):
    Q, K, V = q.astype(np.float64), k.astype(np.float64), v.astype(np.float64)
    y = np.zeros((N, 128, NH * QP))
    for r in range(N):
        for h in range(NH):
            for j in range(N):
                S = np.maximum(K[j][:, 128 * h:128 * h + 128].T @ Q[r][:, QP * h:QP * h + QP], 0.0)
                y[r][:, QP * h:QP * h + QP] += V[j][:, 128 * h:128 * h + 128].T @ S
    return {"y": y.astype(ml_dtypes.bfloat16 if q.dtype != np.float64 else np.float64)}

from concourse.bass import DstId, RemoteDMATransfer
from concourse.mybir import AluOpType

NCORES = 128
NH = 8
B = 128
WAVES = ("k", "q", "v")
NLEAD = 5
LAG = 2
NSB = 6
TIN = {"k": "kin", "q": "qin", "v": "vin"}
LAND = {"k": "kl", "q": "ql", "v": "vl"}

SCRATCH = {
    "kin": ("sbuf", [128, NH * B], "bfloat16"),
    "qin": ("sbuf", [128, NH * B], "bfloat16"),
    "vin": ("sbuf", [128, NH * B], "bfloat16"),
    "rbuf": ("sbuf", [128, 3 * 2 * B], "bfloat16"),
    "kl": ("sbuf", [128, 8 * B], "bfloat16"),
    "ql": ("sbuf", [128, 8 * B], "bfloat16"),
    "vl": ("sbuf", [128, 8 * B], "bfloat16"),
    "sr": ("sbuf", [128, 8 * 8 * B], "bfloat16"),
    "ob": ("sbuf", [128, 8 * B], "bfloat16"),
    "ybuf": ("sbuf", [128, NH * B], "bfloat16"),
    "zero": ("sbuf", [128, 4 * B], "float32"),
    "po0": ("psum", [128, 512], "float32"),
    "po1": ("psum", [128, 512], "float32"),
}
for _i in range(NSB):
    SCRATCH["ps%d" % _i] = ("psum", [128, 512], "float32")

SEMAPHORES = (["ld_k", "ld_q", "ld_v", "own_k", "own_q", "own_v", "h_k", "h_q", "h_v", "k_arr", "v_arr"]
              + ["q_arr%d" % _r for _r in range(8)]
              + ["sent", "zset", "s_done", "relu_done", "o_done", "oc_done", "y0", "y1", "st0", "st1"])


def _bits(mask):
    return [b for b in range(mask.bit_length()) if (mask >> b) & 1]


def _alloc(core, trs, topo):
    allowed = [_bits(topo.mask(core, t["dst"])) for t in trs]
    universe = sorted(set(b for a in allowed for b in a))
    small = [len(a) < len(universe) for a in allowed]
    cap_small = min(len(a) for a in allowed)
    n = len(trs)
    cnt = [1] * n
    grown = True
    while grown:
        grown = False
        lvl = min(cnt)
        for i in range(n):
            if cnt[i] != lvl:
                continue
            tot = sum(cnt) + cnt[i]
            st = sum(c for c, s in zip(cnt, small) if s) + (cnt[i] if small[i] else 0)
            if tot <= len(universe) and st <= cap_small:
                cnt[i] *= 2
                grown = True
    free = list(universe)
    for want_small in (True, False):
        for i in range(n):
            if small[i] != want_small:
                continue
            if want_small:
                take = [b for b in free if b in allowed[i]][:cnt[i]]
            else:
                take = free[len(free) - cnt[i]:]
            free = [b for b in free if b not in take]
            trs[i]["mask"] = sum(1 << b for b in take)
            trs[i]["n"] = cnt[i]


def _plan(cores, topo):
    ranks = list(cores)
    chips = []
    for c in ranks:
        if topo.chip(c) not in chips:
            chips.append(topo.chip(c))
    planes = []
    for x in chips:
        for pl in planes:
            if topo.same_plane(pl[0], x):
                pl.append(x)
                break
        else:
            planes.append([x])
    members = {x: [c for c in range(NCORES) if topo.chip(c) == x] for x in chips}
    rk = {x: [c for c in ranks if topo.chip(c) == x] for x in chips}
    hpp = NH // len(planes)

    def full(c):
        return all(topo.may_write(c, r) for r in ranks if r != c)

    lead, helper, hchip, xsend, ssend = {}, {}, {}, {}, {}
    where = {}
    for pi, pl in enumerate(planes):
        for xi, x in enumerate(pl):
            where[x] = (pi, xi)
            home = topo.die(rk[x][0])
            other = [topo.die(c) for c in members[x] if topo.die(c) != home][0]
            for ds, d in enumerate((home, other)):
                on = [c for c in members[x] if topo.die(c) == d]
                F = sorted([c for c in on if full(c)], key=lambda c: c not in ranks)
                G = [c for c in on if not full(c)]
                h = pi * hpp + ds * len(pl) + xi
                lead[h], helper[h], hchip[h] = F[0], F[1], x
                for pool, tab in ((F, xsend), (G, ssend)):
                    spare = [c for c in pool if c not in ranks]
                    for s in rk[x]:
                        tab[(s, ds)] = s if s in pool else spare.pop(0)

    owner, work = {}, {}
    for h in range(NH):
        x = hchip[h]
        pi, xi = where[x]
        own = sorted([i for i, c in enumerate(ranks) if topo.chip(c) == x], key=lambda i: ranks[i] == lead[h])
        sp = [i for i, c in enumerate(ranks) if topo.chip(c) != x and topo.chip(c) in planes[pi]]
        cr = [i for i, c in enumerate(ranks) if topo.chip(c) not in planes[pi]]
        rot = h % len(cr)
        cr = cr[rot:] + cr[:rot]
        nl = NLEAD - 2
        if NLEAD >= len(ranks):
            mid, rest = cr + sp, []
        else:
            mid, rest = cr[:nl - 1] + sp[:1], cr[nl - 1:] + sp[1:]
        L = [own[0]] + mid + [own[1]]
        work[lead[h]] = (h, L, helper[h] if rest else None)
        if rest:
            work[helper[h]] = (h, rest, None)
        for r in L:
            owner[(h, r)] = lead[h]
        for r in rest:
            owner[(h, r)] = helper[h]

    def dest(t, h, si):
        return owner[(h, si)] if t == "q" else lead[h]

    def asem(t, si):
        return "q_arr%d" % si if t == "q" else t + "_arr"

    calls, local, relay = {}, {}, {}
    for si, cs in enumerate(ranks):
        x = topo.chip(cs)
        pi, xi = where[x]
        npl = len(planes[pi])
        for w, t in enumerate(WAVES):
            wide, hand, off, land = [], [], [], []
            for ds in (0, 1):
                groups = []
                for po in range(len(planes)):
                    if po != pi:
                        h0 = po * hpp + ds * len(planes[po])
                        groups.append((xsend[(cs, ds)], [h0 + i for i in range(len(planes[po]))]))
                for xo in range(npl):
                    if xo != xi:
                        groups.append((ssend[(cs, ds)], [pi * hpp + ds * npl + xo]))
                for snd, heads in groups:
                    outs = []
                    for i, h in enumerate(heads):
                        if snd == cs:
                            src = (TIN[t], h * B, (h + 1) * B)
                        else:
                            src = ("rbuf", (2 * w + i) * B, (2 * w + i + 1) * B)
                        outs.append({"dst": dest(t, h, si), "sem": asem(t, si), "src": src,
                                     "dap": (LAND[t], si * B, (si + 1) * B)})
                    if snd == cs:
                        off += outs
                    else:
                        tr = {"dst": snd, "sem": "h_" + t, "src": (TIN[t], heads[0] * B, (heads[-1] + 1) * B),
                              "dap": ("rbuf", 2 * w * B, (2 * w + len(heads)) * B)}
                        (wide if len(heads) > 1 else hand).append(tr)
                        relay.setdefault(snd, []).append({"wait": ["h_" + t], "trs": outs})
                ho = pi * hpp + ds * npl + xi
                d = dest(t, ho, si)
                if d == cs:
                    local.setdefault(cs, []).append((t, ho, si))
                else:
                    land.append({"dst": d, "sem": asem(t, si), "src": (TIN[t], ho * B, (ho + 1) * B),
                                 "dap": (LAND[t], si * B, (si + 1) * B)})
            for trs in (wide, hand + off + land):
                if trs:
                    calls.setdefault(cs, []).append({"wait": ["ld_" + t], "trs": trs})
    for c, cl in relay.items():
        calls.setdefault(c, []).extend(cl)

    exp, sent = {}, {}

    def add(src, dst, sem, n):
        exp[(dst, sem)] = exp.get((dst, sem), 0) + n
        sent[src] = sent.get(src, 0) + n

    for c, cl in calls.items():
        for call in cl:
            _alloc(c, call["trs"], topo)
            for tr in call["trs"]:
                add(c, tr["dst"], tr["sem"], tr["n"])
    for c, (h, rl, peer) in work.items():
        if peer is not None:
            for t in ("k", "v"):
                add(c, peer, t + "_arr", len(_bits(topo.mask(c, peer))))
        for r in rl:
            if ranks[r] != c:
                add(c, ranks[r], "y%d" % (h // hpp), len(_bits(topo.mask(c, ranks[r]))))
    return {"ranks": ranks, "calls": calls, "local": local, "work": work, "exp": exp, "sent": sent, "hpp": hpp}


def _compute(g, core, T, P):
    sem = T.sem
    h, rl, _peer = P["work"][core]
    ranks, exp = P["ranks"], P["exp"]
    mine = P["local"].get(core, [])
    m = len(rl)
    te, ve = g.tensor, g.vector
    ps = [T["ps%d" % i] for i in range(NSB)]
    po = [T.po0, T.po1]

    def wait_in(q, t, name):
        if exp.get((core, name), 0):
            q.wait_ge(sem[name], exp[(core, name)])
        if t != "q" and any(x[0] == t for x in mine):
            q.wait_ge(sem["own_" + t], 16)

    ve.memset(T.zero[:, :], 0.0).then_inc(sem.zset, 1)
    ve.wait_ge(sem.zset, 1)
    for i in range(m + LAG):
        if i < m:
            r = rl[i]
            if i == 0:
                wait_in(te, "k", "k_arr")
            if any(x[0] == "q" and x[2] == r for x in mine):
                te.wait_ge(sem.own_q, 16)
            else:
                te.wait_ge(sem["q_arr%d" % r], exp[(core, "q_arr%d" % r)])
            for half in (0, 1):
                u = 2 * i + half
                if u >= NSB:
                    te.wait_ge(sem.relu_done, u - NSB + 1)
                for jj in range(4):
                    j = 4 * half + jj
                    te.matmul(ps[u % NSB][:, jj * B:(jj + 1) * B], T.kl[:, j * B:(j + 1) * B],
                              T.ql[:, r * B:(r + 1) * B], start=True, stop=True).then_inc(sem.s_done, 1)
                ve.wait_ge(sem.s_done, 4 * (u + 1))
                ve.tensor_tensor(T.sr[:, u * 4 * B:(u + 1) * 4 * B], ps[u % NSB][:, :], T.zero[:, :],
                                 AluOpType.max).then_inc(sem.relu_done, 1)
        if i >= LAG:
            o = i - LAG
            r = rl[o]
            if o == 0:
                wait_in(te, "v", "v_arr")
            te.wait_ge(sem.relu_done, 2 * o + 2)
            if o >= 2:
                te.wait_ge(sem.oc_done, o - 1)
            for j in range(8):
                te.matmul(po[o % 2][:, 0:B], T.vl[:, j * B:(j + 1) * B], T.sr[:, (8 * o + j) * B:(8 * o + j + 1) * B],
                          start=(j == 0), stop=(j == 7)).then_inc(sem.o_done, 1)
            ve.wait_ge(sem.o_done, 8 * (o + 1))
            out = T.ybuf[:, h * B:(h + 1) * B] if ranks[r] == core else T.ob[:, o * B:(o + 1) * B]
            ve.tensor_copy(out, po[o % 2][:, 0:B]).then_inc(sem.oc_done, 1)


def rank_program(g, core, T, topo):
    P = _plan(T.cores, topo)
    ranks, exp, hpp = P["ranks"], P["exp"], P["hpp"]
    sem = T.sem
    is_rank = core in ranks
    job = P["work"].get(core)
    if not (is_rank or job or core in P["calls"]):
        return
    mine = P["local"].get(core, [])

    if is_rank:
        g.sync.dma_start(T.kin[:, :], T.k[:, :]).then_inc(sem.ld_k, 16)
        g.scalar.dma_start(T.qin[:, :], T.q[:, :]).then_inc(sem.ld_q, 16)
        g.sync.dma_start(T.vin[:, :], T.v[:, :]).then_inc(sem.ld_v, 16)
        for n, (t, h, si) in enumerate(mine):
            qd = g.scalar if n % 2 == 0 else g.sync
            qd.dma_start(T[LAND[t]][:, si * B:(si + 1) * B], T[t][:, h * B:(h + 1) * B]).then_inc(sem["own_" + t], 16)

    if job:
        _compute(g, core, T, P)

    waited = set()
    for call in P["calls"].get(core, []):
        for w in call["wait"]:
            if w not in waited:
                g.wait_ge(sem[w], 16 if w.startswith("ld_") else exp[(core, w)])
                waited.add(w)
        trs = []
        for tr in call["trs"]:
            rid, pid, _se = topo.addr(tr["dst"])
            sn, s0, s1 = tr["src"]
            dn, d0, d1 = tr["dap"]
            trs.append(RemoteDMATransfer(dst_ids=[DstId(rid=rid, pnc=pid)], dma_engine_mask=tr["mask"],
                                         remote_sem=sem[tr["sem"]], src=T[sn][:, s0:s1], dst=T[dn][:, d0:d1]))
        g.remote_dma_fused(trs, local_sem=sem.sent)

    if job:
        h, rl, peer = job
        if peer is not None:
            rid, pid, _se = topo.addr(peer)
            for t in ("k", "v"):
                g.wait_ge(sem[t + "_arr"], exp[(core, t + "_arr")])
                if any(x[0] == t for x in mine):
                    g.wait_ge(sem["own_" + t], 16)
                g.remote_dma(out_ap=T[LAND[t]][:, :], in_ap=T[LAND[t]][:, :], remote_sem=sem[t + "_arr"],
                             local_sem=sem.sent, pid=pid, routing_id=rid, dma_engine_mask=topo.mask(core, peer))
        for o, r in enumerate(rl):
            g.wait_ge(sem.oc_done, o + 1)
            if ranks[r] == core:
                continue
            rid, pid, _se = topo.addr(ranks[r])
            g.remote_dma(out_ap=T.ybuf[:, h * B:(h + 1) * B], in_ap=T.ob[:, o * B:(o + 1) * B],
                         remote_sem=sem["y%d" % (h // hpp)], local_sem=sem.sent, pid=pid, routing_id=rid,
                         dma_engine_mask=topo.mask(core, ranks[r]))

    if is_rank:
        for a, qd in enumerate((g.sync, g.scalar)):
            qd.wait_ge(sem["y%d" % a], exp[(core, "y%d" % a)])
            if job and job[0] // hpp == a and core in [ranks[r] for r in job[1]]:
                qd.wait_ge(sem.oc_done, len(job[1]))
            c0, c1 = a * hpp * B, (a + 1) * hpp * B
            qd.dma_start(T.y[:, c0:c1], T.ybuf[:, c0:c1]).then_inc(sem["st%d" % a], 16)
        g.wait_ge(sem.st0, 16)
        g.wait_ge(sem.st1, 16)
    if P["sent"].get(core, 0):
        g.wait_ge(sem.sent, P["sent"][core])
